import numpy as np
import ml_dtypes


def mxq(x, axis, fmt="e4m3"):
    dtype, down = {"e4m3": (ml_dtypes.float8_e4m3fn, 7), "e5m2": (ml_dtypes.float8_e5m2, 14)}[fmt]
    v = np.moveaxis(np.asarray(x, np.float32).astype(ml_dtypes.bfloat16).astype(np.float64), axis, -1)
    blocks = v.reshape(v.shape[:-1] + (-1, 32))
    amax = np.abs(blocks).max(-1, keepdims=True)
    byte = np.maximum(np.where(amax > 0, np.frexp(amax)[1] - 1 + 127, 0) - down, 1)
    scale = np.exp2(byte - 127.0)
    codes = (blocks / scale).astype(np.float32).astype(dtype).astype(np.float64)
    return np.moveaxis((codes * scale).reshape(v.shape), -1, axis)


WIDE = False


def mx_kscale(k):
    if not WIDE:
        return np.ones(k)
    levels = np.array([10, -10, 5, -5, 0])
    if k % 512:
        return np.exp2(np.random.permutation(np.resize(levels, k // 32))).repeat(32)
    a = np.empty((k // 512, 16))
    for p in range(k // 512):
        a[p, :8] = np.random.permutation(np.resize(levels, 8))
        for g in range(8):
            far = levels[np.abs(levels - a[p, g]) >= 10]
            a[p, g + 8] = far[np.random.randint(len(far))]
    return np.exp2(a.ravel()).repeat(32)


BF16 = ml_dtypes.bfloat16


def bf(x):
    return np.asarray(x, np.float32).astype(BF16)


def f64(x):
    return np.asarray(x).astype(np.float64)


E2M1 = np.array([0.0, 0.5, 1.0, 1.5, 2.0, 3.0, 4.0, 6.0, -0.0, -0.5, -1.0, -1.5, -2.0, -3.0, -4.0, -6.0])


def pack_weight(w, fmt):
    k, n = w.shape
    w = f64(bf(w)).reshape(k // 32, 32, n)
    amax = np.abs(w).max(1)
    if fmt == "e4m3":
        byte = np.frexp(amax)[1] - 1 + 127 - 7
    else:
        mant, ex = np.frexp(amax / 6.0)
        byte = np.where(mant > 0.5, ex, ex - 1) + 127
    byte = np.clip(np.where(amax > 0, byte, 1), 1, 254)
    scaled = (w * np.exp2(127.0 - byte)[:, None, :]).reshape(k, n).astype(np.float32)
    by_word = np.ascontiguousarray(scaled.reshape(k // 512, 128, 4, n).transpose(0, 1, 3, 2))
    if fmt == "e4m3":
        words = by_word.astype(ml_dtypes.float8_e4m3fn).view(np.uint8)
    else:
        c = by_word.astype(ml_dtypes.float4_e2m1fn).view(np.uint8) & 0xF
        words = c[..., 0::2] | (c[..., 1::2] << 4)
    return np.ascontiguousarray(words), np.ascontiguousarray(byte.astype(np.uint8).reshape(k // 512, 16, n))


def unpack_weight(words, scales, fmt):
    g, p, n, _ = words.shape
    if fmt == "e4m3":
        vals = np.ascontiguousarray(words).view(ml_dtypes.float8_e4m3fn).astype(np.float64)
    else:
        nib = np.empty((g, p, n, 4), np.uint8)
        nib[..., 0::2] = words & 0xF
        nib[..., 1::2] = words >> 4
        vals = E2M1[nib]
    vals = vals * np.repeat(np.exp2(scales.astype(np.float64) - 127.0), 8, axis=1)[..., None]
    return vals.transpose(0, 1, 3, 2).reshape(g * 512, n)
def pack4(w):
    words, scales = pack_weight(w, "e2m1")
    return words.reshape(words.shape[0], 128, -1), scales


def unpack4(words, scales):
    return unpack_weight(words.reshape(words.shape[0], 128, -1, 2), scales, "e2m1")


I, A, K, F, C = 2048, 1024, 1024, 512, 512


def setup_inputs():
    s = mx_kscale(K)
    r = mx_kscale(F)
    t = mx_kscale(I)
    price = 0.5 * np.abs(np.random.standard_normal((I, A)))
    w = 0.7 * np.random.standard_normal((K, A)) / np.sqrt(K) / s[:, None]
    w_words, w_scales = pack4(w)
    return {"x": bf(np.random.standard_normal((I, K)) * s),
            "w_words": w_words,
            "w_scales": w_scales,
            "discount": bf(np.exp(-price) / I ** 0.25 * t[:, None]),
            "z": bf(np.random.standard_normal((I, F)) / I ** 0.25 * r / t[:, None]),
            "v": bf(np.random.standard_normal((F, C)) / np.sqrt(F) / r[:, None]),
            "budget": bf(np.abs(np.random.standard_normal((A, C))))}


def reference(x, w_words, w_scales, discount, z, v, budget):
    bids = mxq(f64(x), 1, "e4m3") @ unpack4(w_words, w_scales)
    alloc = np.exp(bids) * f64(discount)
    costs = mxq(f64(z), 1, "e4m3") @ mxq(f64(v), 0, "e4m3")
    spend = mxq(alloc, 0, "e4m3").T @ mxq(costs, 0, "e4m3")
    return spend - f64(budget)

@@ -1,0 +1,302 @@
+from contextlib import ExitStack
+
+import concourse.mybir as mybir
+from concourse.masks import make_identity
+
+I, A, K, F, C = 2048, 1024, 1024, 512, 512
+FLOPS = 2 * I * K * A + 2 * I * F * C + 2 * I * A * C
+
+F32 = mybir.dt.float32
+BF16 = mybir.dt.bfloat16
+U32 = mybir.dt.uint32
+I32 = mybir.dt.int32
+U8 = mybir.dt.uint8
+FP8X4 = mybir.dt.float8_e4m3fn_x4
+FP4X4 = mybir.dt.float4_e2m1fn_x4
+EXP = mybir.ActivationFunctionType.Exp
+MULT = mybir.AluOpType.mult
+SUB = mybir.AluOpType.subtract
+
+P = 128
+PACK = 4
+PASS = P * PACK
+BANK = 512
+GROUPS = I // PASS
+K_PASSES = K // PASS
+HALVES = A // BANK
+A_TILES = BANK // P
+C_TILES = C // P
+RUN = 4
+
+
+def tile_ad_allocation_dual_s11_kernel(tc, x, w_words, w_scales, discount, z, v, budget, out):
+    nc = tc.nc
+    with ExitStack() as ctx:
+        keep = ctx.enter_context(tc.tile_pool(name="keep", bufs=1))
+        stage = ctx.enter_context(tc.tile_pool(name="stage", bufs=4))
+        psum = ctx.enter_context(tc.psum_pool(name="psum", bufs=8))
+        ctx.enter_context(tc.manual_schedule())
+
+        def kept(name, shape, dtype):
+            return keep.tile(shape, dtype, name=name, align_bytes=64)
+
+        def staged(name, shape, dtype, bufs):
+            return stage.tile(shape, dtype, name=name, bufs=bufs, align_bytes=64)
+
+        def new_bank():
+            return psum.tile([P, BANK], F32, name="bank")
+
+        def quantize(name, grouped):
+            width = grouped.shape[1] // PACK
+            codes = kept(name + "_codes", [P, width], U32)
+            scales = kept(name + "_scales", [P, width], U8)
+            nc.vector.quantize_mx(out=codes[:].bitcast(FP8X4), scales=scales[:], in_=grouped)
+            return codes, scales
+
+        ident = kept("ident", [P, P], F32)
+        make_identity(nc, ident[:])
+        w_plane = kept("w_plane", [P, K_PASSES * A], U8)
+        nc.vector.memset(w_plane[:].bitcast(I32), 0)
+        warm = kept("warm", [P, 1], F32)
+        nc.scalar.activation(out=warm[:], in_=ident[:, 0:1], func=EXP)
+
+        x_raw, z_raw, d_raw, w_raw, b_raw = {}, {}, {}, {}, {}
+        x_rows = x.rearrange("(g m t) k -> g m t k", m=P, t=PACK)
+        z_rows = z.rearrange("(g m t) f -> g m t f", m=P, t=PACK)
+        d_rows = discount.rearrange("(g m t) a -> g m t a", m=P, t=PACK)
+
+        def load_x(g, t0, n):
+            raw = kept("x_raw%d_%d" % (g, t0), [P, n, K], BF16)
+            nc.sync.dma_start(out=raw[:], in_=x_rows[g, :, t0:t0 + n, :])
+            for t in range(n):
+                x_raw[g, t0 + t] = raw[:, t, :]
+
+        def load_z(g):
+            z_raw[g] = kept("z_raw%d" % g, [P, PACK, F], BF16)
+            nc.sync.dma_start(out=z_raw[g][:], in_=z_rows[g])
+
+        def load_d(g, h):
+            d_raw[g, h] = kept("d_raw%d_%d" % (g, h), [P, PACK, BANK], BF16)
+            nc.sync.dma_start(out=d_raw[g, h][:], in_=d_rows[g, :, :, h * BANK:(h + 1) * BANK])
+
+        def load_w(h):
+            w_raw[h] = kept("w_raw%d" % h, [P, K_PASSES, 2 * BANK], U8)
+            src = w_words.rearrange("g p n -> p g n")[:, :, 2 * h * BANK:2 * (h + 1) * BANK]
+            nc.sync.dma_start(out=w_raw[h][:].bitcast(I32), in_=src.bitcast(I32))
+
+        def load_w_scales():
+            src = w_scales.rearrange("g (q r) n -> r q g n", r=PACK)
+            for r in range(PACK):
+                dst = w_plane[r:P:32, :].rearrange("q (g n) -> q g n", g=K_PASSES)
+                nc.sync.dma_start(out=dst.bitcast(I32), in_=src[r].bitcast(I32))
+
+        def load_budget(h):
+            b_raw[h] = kept("b_raw%d" % h, [P, A_TILES, C], BF16)
+            src = budget[h * BANK:(h + 1) * BANK, :].rearrange("(j m) c -> m j c", m=P)
+            nc.sync.dma_start(out=b_raw[h][:], in_=src)
+
+        load_x(0, 0, 1)
+        load_x(0, 1, 1)
+        load_x(0, 2, 2)
+        load_w(0)
+        load_w_scales()
+        v_raw = kept("v_raw", [P, PACK, C], BF16)
+        nc.sync.dma_start(out=v_raw[:], in_=v.rearrange("(p j) c -> p j c", j=PACK))
+        load_z(0)
+        load_z(1)
+        load_w(1)
+        load_d(0, 0)
+        load_x(1, 0, 2)
+        load_x(1, 2, 2)
+        load_d(0, 1)
+        for g in range(2, GROUPS):
+            load_z(g)
+            load_d(g - 1, 0)
+            load_x(g, 0, 2)
+            load_x(g, 2, 2)
+            load_d(g - 1, 1)
+        load_d(GROUPS - 1, 0)
+        load_d(GROUPS - 1, 1)
+        load_budget(0)
+        load_budget(1)
+
+        xq, zq, cq, aq = {}, {}, {}, {}
+        x_grp, z_grp, c_grp, e_val, a_grp = {}, {}, {}, {}, {}
+
+        def copy_on(engine, out_ap, in_ap):
+            if engine == "s":
+                nc.scalar.copy(out=out_ap, in_=in_ap)
+            else:
+                nc.vector.tensor_copy(out=out_ap, in_=in_ap)
+
+        def turn_x(g, t):
+            bank = new_bank()
+            words = x_raw[g, t].bitcast(F32)
+            for kp in range(K_PASSES):
+                for u in range(2):
+                    n = 2 * kp + u
+                    nc.tensor.transpose(bank[:, n * P:(n + 1) * P], words[:, 256 * kp + u:256 * (kp + 1):2], ident[:])
+            return bank
+
+        def turn_z(g, pair):
+            bank = new_bank()
+            words = z_raw[g][:].rearrange("p t f -> p (t f)").bitcast(F32)
+            for tt in range(2):
+                t = 2 * pair + tt
+                for u in range(2):
+                    n = 2 * tt + u
+                    nc.tensor.transpose(bank[:, n * P:(n + 1) * P], words[:, 256 * t + u:256 * (t + 1):2], ident[:])
+            return bank
+
+        def drain_words(engine, bank, name):
+            grouped = staged(name, [P, 2 * BANK], BF16, 5)
+            copy_on(engine, grouped[:].bitcast(F32).rearrange("p (n m u) -> p n m u", n=2, u=2),
+                    bank[:].rearrange("p (n u m) -> p n m u", n=2, u=2))
+            return grouped
+
+        def quant_x(g, t):
+            xq[g, t] = quantize("xq%d_%d" % (g, t), x_grp[g, t][:])
+
+        def quant_z(g, pair):
+            zq[g, pair] = quantize("zq%d_%d" % (g, pair), z_grp[g, pair][:])
+
+        def bids(g, h, t):
+            bank = new_bank()
+            codes, scales = xq[g, t]
+            for kp in range(K_PASSES):
+                cols = slice(kp * P, (kp + 1) * P)
+                nc.tensor.matmul_mx(
+                    out=bank[:], lhsT=codes[:, cols].bitcast(FP8X4), lhsT_scale=scales[:, cols],
+                    rhs=w_raw[h][:, kp, :].bitcast(FP4X4),
+                    rhs_scale=w_plane[:, kp * A + h * BANK:kp * A + (h + 1) * BANK],
+                    start=(kp == 0), stop=(kp == K_PASSES - 1))
+            if t == 0:
+                e_val[g, h] = staged("e_val", [P, PACK, BANK], F32, 3)
+            nc.scalar.activation(out=e_val[g, h][:, t, :], in_=bank[:], func=EXP)
+
+        def weigh(g, h, a0, n):
+            grouped = staged("a_grp", [P, n * PACK], BF16, 4)
+            a_grp[g, h, a0] = grouped
+            nc.vector.tensor_tensor(
+                out=grouped[:].rearrange("p (c i t) -> p c t i", i=RUN, t=PACK),
+                in0=e_val[g, h][:, :, a0:a0 + n].rearrange("p t (c i) -> p c t i", i=RUN),
+                in1=d_raw[g, h][:, :, a0:a0 + n].rearrange("p t (c i) -> p c t i", i=RUN),
+                op=MULT)
+
+        def quant_a(g, h, a0):
+            codes, scales = quantize("aq%d_%d_%d" % (g, h, a0), a_grp[g, h, a0][:])
+            for m0 in range(0, codes.shape[1], P):
+                aq[g, (h * BANK + a0 + m0) // P] = (codes[:, m0:m0 + P], scales[:, m0:m0 + P])
+
+        def costs(g, cc):
+            bank = new_bank()
+            v_codes, v_scales = vq
+            cols = slice(cc * P, (cc + 1) * P)
+            for t in range(PACK):
+                codes, scales = zq[g, t // 2]
+                rows = slice((t % 2) * P, (t % 2 + 1) * P)
+                nc.tensor.matmul_mx(
+                    out=bank[:, t * P:(t + 1) * P], lhsT=codes[:, rows].bitcast(FP8X4), lhsT_scale=scales[:, rows],
+                    rhs=v_codes[:, cols].bitcast(FP8X4), rhs_scale=v_scales[:, cols], start=True, stop=True)
+            return bank
+
+        def drain_costs(engine, g, cc, bank):
+            if cc == 0:
+                c_grp[g] = staged("c_grp", [P, C * PACK], BF16, 2)
+            copy_on(engine, c_grp[g][:, cc * BANK:(cc + 1) * BANK].rearrange("p (n t) -> p n t", t=PACK),
+                    bank[:].rearrange("p (t n) -> p n t", t=PACK))
+
+        def quant_c(g):
+            cq[g] = quantize("cq%d" % g, c_grp[g][:])
+
+        def spend_pass(bank, j, g):
+            a_codes, a_scales = aq[g, j]
+            c_codes, c_scales = cq[g]
+            nc.tensor.matmul_mx(
+                out=bank[:], lhsT=a_codes.bitcast(FP8X4), lhsT_scale=a_scales,
+                rhs=c_codes[:].bitcast(FP8X4), rhs_scale=c_scales[:],
+                start=(g == 0), stop=(g == GROUPS - 1))
+
+        def finish(bank, j):
+            res = staged("res", [P, C], F32, 4)
+            nc.vector.tensor_tensor(out=res[:], in0=bank[:], in1=b_raw[j // A_TILES][:, j % A_TILES, :], op=SUB)
+            nc.sync.dma_start(out=out[j * P:(j + 1) * P, :], in_=res[:])
+
+        HALF = BANK // 2
+        last = GROUPS - 1
+
+        def turn_and_drain_x(engine, g, t):
+            x_grp[g, t] = drain_words(engine, turn_x(g, t), "grp")
+
+        def turn_and_drain_z(engine, g, pair):
+            z_grp[g, pair] = drain_words(engine, turn_z(g, pair), "grp")
+
+        for t in range(PACK):
+            turn_and_drain_x("s" if t % 2 else "v", 0, t)
+            if t > 0:
+                quant_x(0, t - 1)
+        quant_x(0, 3)
+        for t in range(PACK):
+            bids(0, 0, t)
+        v_grp = kept("v_grp", [P, C * PACK], BF16)
+        nc.vector.tensor_copy(
+            out=v_grp[:].rearrange("p (c i t) -> p c t i", i=RUN, t=PACK),
+            in_=v_raw[:].rearrange("p t (c i) -> p c t i", i=RUN))
+        turn_and_drain_z("v", 0, 0)
+        vq = quantize("vq", v_grp[:])
+        turn_and_drain_z("v", 0, 1)
+        quant_z(0, 0)
+        quant_z(0, 1)
+
+        for g in range(1, GROUPS):
+            for pair in range(2):
+                turn_and_drain_z("s", g, pair)
+            weigh(g - 1, 0, 0, HALF)
+            weigh(g - 1, 0, HALF, HALF)
+            quant_z(g, 0)
+            quant_z(g, 1)
+            quant_a(g - 1, 0, 0)
+            quant_a(g - 1, 0, HALF)
+            for t in range(PACK):
+                bids(g - 1, 1, t)
+            for t in range(PACK):
+                turn_and_drain_x("s", g, t)
+            weigh(g - 1, 1, 0, HALF)
+            quant_x(g, 0)
+            quant_x(g, 1)
+            if g == 1:
+                for cc in range(C_TILES):
+                    drain_costs("s", 0, cc, costs(0, cc))
+            weigh(g - 1, 1, HALF, HALF)
+            for cc in range(C_TILES):
+                if cc == 1:
+                    quant_x(g, 2)
+                    quant_x(g, 3)
+                drain_costs("v" if cc % 2 else "s", g, cc, costs(g, cc))
+            quant_a(g - 1, 1, 0)
+            quant_a(g - 1, 1, HALF)
+            if g == 1:
+                quant_c(0)
+            quant_c(g)
+            for t in range(PACK):
+                bids(g, 0, t)
+
+        weigh(last, 0, 0, HALF)
+        weigh(last, 0, HALF, HALF)
+        quant_a(last, 0, 0)
+        quant_a(last, 0, HALF)
+        for t in range(PACK):
+            bids(last, 1, t)
+        banks = [new_bank(), new_bank()]
+        for j in range(2):
+            for g in range(last):
+                spend_pass(banks[j], j, g)
+        for j in range(HALVES * A_TILES):
+            if j < A_TILES:
+                weigh(last, 1, j * P, P)
+            if 0 < j <= A_TILES:
+                quant_a(last, 1, (j - 1) * P)
+            bank = banks[j] if j < 2 else new_bank()
+            for g in range(last if j < 2 else 0, GROUPS):
+                spend_pass(bank, j, g)
+            finish(bank, j)

@@ -27,6 +27,8 @@ HALVES = A // BANK
 A_TILES = BANK // P
 C_TILES = C // P
 RUN = 4
+CE0 = "svsv"
+CE = ["", "svsv", "svsv", "svss"]
 
 
 def tile_ad_allocation_dual_s11_kernel(tc, x, w_words, w_scales, discount, z, v, budget, out):
@@ -46,10 +48,10 @@ def tile_ad_allocation_dual_s11_kernel(tc, x, w_words, w_scales, discount, z, v,
         def new_bank():
             return psum.tile([P, BANK], F32, name="bank")
 
-        def quantize(name, grouped):
+        def quantize(name, grouped, bufs=1):
             width = grouped.shape[1] // PACK
-            codes = kept(name + "_codes", [P, width], U32)
-            scales = kept(name + "_scales", [P, width], U8)
+            codes = staged(name + "_codes", [P, width], U32, bufs)
+            scales = staged(name + "_scales", [P, width], U8, bufs)
             nc.vector.quantize_mx(out=codes[:].bitcast(FP8X4), scales=scales[:], in_=grouped)
             return codes, scales
 
@@ -57,8 +59,6 @@ def tile_ad_allocation_dual_s11_kernel(tc, x, w_words, w_scales, discount, z, v,
         make_identity(nc, ident[:])
         w_plane = kept("w_plane", [P, K_PASSES * A], U8)
         nc.vector.memset(w_plane[:].bitcast(I32), 0)
-        warm = kept("warm", [P, 1], F32)
-        nc.scalar.activation(out=warm[:], in_=ident[:, 0:1], func=EXP)
 
         x_raw, z_raw, d_raw, w_raw, b_raw = {}, {}, {}, {}, {}
         x_rows = x.rearrange("(g m t) k -> g m t k", m=P, t=PACK)
@@ -97,25 +97,21 @@ def tile_ad_allocation_dual_s11_kernel(tc, x, w_words, w_scales, discount, z, v,
 
         load_x(0, 0, 1)
         load_x(0, 1, 1)
-        load_x(0, 2, 2)
+        load_x(0, 2, 1)
+        load_x(0, 3, 1)
         load_w(0)
         load_w_scales()
         v_raw = kept("v_raw", [P, PACK, C], BF16)
         nc.sync.dma_start(out=v_raw[:], in_=v.rearrange("(p j) c -> p j c", j=PACK))
         load_z(0)
-        load_z(1)
-        load_w(1)
         load_d(0, 0)
-        load_x(1, 0, 2)
-        load_x(1, 2, 2)
-        load_d(0, 1)
-        for g in range(2, GROUPS):
-            load_z(g)
-            load_d(g - 1, 0)
+        load_w(1)
+        for g in range(1, GROUPS):
             load_x(g, 0, 2)
             load_x(g, 2, 2)
             load_d(g - 1, 1)
-        load_d(GROUPS - 1, 0)
+            load_z(g)
+            load_d(g, 0)
         load_d(GROUPS - 1, 1)
         load_budget(0)
         load_budget(1)
@@ -148,17 +144,18 @@ def tile_ad_allocation_dual_s11_kernel(tc, x, w_words, w_scales, discount, z, v,
                     nc.tensor.transpose(bank[:, n * P:(n + 1) * P], words[:, 256 * t + u:256 * (t + 1):2], ident[:])
             return bank
 
-        def drain_words(engine, bank, name):
-            grouped = staged(name, [P, 2 * BANK], BF16, 5)
-            copy_on(engine, grouped[:].bitcast(F32).rearrange("p (n m u) -> p n m u", n=2, u=2),
+        def drain_words(engine, bank, grouped):
+            copy_on(engine, grouped.bitcast(F32).rearrange("p (n m u) -> p n m u", n=2, u=2),
                     bank[:].rearrange("p (n u m) -> p n m u", n=2, u=2))
-            return grouped
 
-        def quant_x(g, t):
-            xq[g, t] = quantize("xq%d_%d" % (g, t), x_grp[g, t][:])
+        def quant_x(g, t0):
+            codes, scales = quantize("xq%d_%d" % (g, t0), x_grp[g, t0][:])
+            width = K_PASSES * P
+            for c0 in range(0, codes.shape[1], width):
+                xq[g, t0 + c0 // width] = (codes[:, c0:c0 + width], scales[:, c0:c0 + width])
 
-        def quant_z(g, pair):
-            zq[g, pair] = quantize("zq%d_%d" % (g, pair), z_grp[g, pair][:])
+        def quant_z(g):
+            zq[g] = quantize("zq", z_grp[g][:], 2)
 
         def bids(g, h, t):
             bank = new_bank()
@@ -175,7 +172,7 @@ def tile_ad_allocation_dual_s11_kernel(tc, x, w_words, w_scales, discount, z, v,
             nc.scalar.activation(out=e_val[g, h][:, t, :], in_=bank[:], func=EXP)
 
         def weigh(g, h, a0, n):
-            grouped = staged("a_grp", [P, n * PACK], BF16, 4)
+            grouped = staged("a_grp", [P, n * PACK], BF16, 3)
             a_grp[g, h, a0] = grouped
             nc.vector.tensor_tensor(
                 out=grouped[:].rearrange("p (c i t) -> p c t i", i=RUN, t=PACK),
@@ -193,8 +190,8 @@ def tile_ad_allocation_dual_s11_kernel(tc, x, w_words, w_scales, discount, z, v,
             v_codes, v_scales = vq
             cols = slice(cc * P, (cc + 1) * P)
             for t in range(PACK):
-                codes, scales = zq[g, t // 2]
-                rows = slice((t % 2) * P, (t % 2 + 1) * P)
+                codes, scales = zq[g]
+                rows = slice(t * P, (t + 1) * P)
                 nc.tensor.matmul_mx(
                     out=bank[:, t * P:(t + 1) * P], lhsT=codes[:, rows].bitcast(FP8X4), lhsT_scale=scales[:, rows],
                     rhs=v_codes[:, cols].bitcast(FP8X4), rhs_scale=v_scales[:, cols], start=True, stop=True)
@@ -209,94 +206,122 @@ def tile_ad_allocation_dual_s11_kernel(tc, x, w_words, w_scales, discount, z, v,
         def quant_c(g):
             cq[g] = quantize("cq%d" % g, c_grp[g][:])
 
-        def spend_pass(bank, j, g):
+        def spend_pass(bank, j, g, c0=0, n=C):
             a_codes, a_scales = aq[g, j]
             c_codes, c_scales = cq[g]
             nc.tensor.matmul_mx(
-                out=bank[:], lhsT=a_codes.bitcast(FP8X4), lhsT_scale=a_scales,
-                rhs=c_codes[:].bitcast(FP8X4), rhs_scale=c_scales[:],
+                out=bank[:, 0:n], lhsT=a_codes.bitcast(FP8X4), lhsT_scale=a_scales,
+                rhs=c_codes[:, c0:c0 + n].bitcast(FP8X4), rhs_scale=c_scales[:, c0:c0 + n],
                 start=(g == 0), stop=(g == GROUPS - 1))
 
-        def finish(bank, j):
-            res = staged("res", [P, C], F32, 4)
-            nc.vector.tensor_tensor(out=res[:], in0=bank[:], in1=b_raw[j // A_TILES][:, j % A_TILES, :], op=SUB)
-            nc.sync.dma_start(out=out[j * P:(j + 1) * P, :], in_=res[:])
+        def finish(bank, j, c0=0, n=C):
+            res = staged("res", [P, n], F32, 8)
+            nc.vector.tensor_tensor(out=res[:], in0=bank[:, 0:n], in1=b_raw[j // A_TILES][:, j % A_TILES, c0:c0 + n], op=SUB)
+            nc.sync.dma_start(out=out[j * P:(j + 1) * P, c0:c0 + n], in_=res[:])
 
         HALF = BANK // 2
         last = GROUPS - 1
 
-        def turn_and_drain_x(engine, g, t):
-            x_grp[g, t] = drain_words(engine, turn_x(g, t), "grp")
+        def turn_and_drain_x(engine, g, t0, n):
+            x_grp[g, t0] = staged("grp", [P, n * K], BF16, 4)
+            for t in range(n):
+                drain_words(engine, turn_x(g, t0 + t), x_grp[g, t0][:, t * K:(t + 1) * K])
 
         def turn_and_drain_z(engine, g, pair):
-            z_grp[g, pair] = drain_words(engine, turn_z(g, pair), "grp")
+            if pair == 0:
+                z_grp[g] = staged("grp", [P, 4 * BANK], BF16, 4)
+            drain_words(engine, turn_z(g, pair), z_grp[g][:, pair * 2 * BANK:(pair + 1) * 2 * BANK])
+
+        def all_bids(g, h):
+            for t in range(PACK):
+                bids(g, h, t)
+
+        def all_costs(g, engines):
+            for cc in range(C_TILES):
+                drain_costs(engines[cc], g, cc, costs(g, cc))
 
         for t in range(PACK):
-            turn_and_drain_x("s" if t % 2 else "v", 0, t)
-            if t > 0:
+            turn_and_drain_x("v", 0, t, 1)
+            if t % 2:
                 quant_x(0, t - 1)
-        quant_x(0, 3)
-        for t in range(PACK):
-            bids(0, 0, t)
-        v_grp = kept("v_grp", [P, C * PACK], BF16)
+                quant_x(0, t)
+        all_bids(0, 0)
+        v_grp = staged("grp", [P, C * PACK], BF16, 4)
         nc.vector.tensor_copy(
             out=v_grp[:].rearrange("p (c i t) -> p c t i", i=RUN, t=PACK),
             in_=v_raw[:].rearrange("p t (c i) -> p c t i", i=RUN))
-        turn_and_drain_z("v", 0, 0)
+        turn_and_drain_z("s", 0, 0)
+        turn_and_drain_z("s", 0, 1)
         vq = quantize("vq", v_grp[:])
-        turn_and_drain_z("v", 0, 1)
-        quant_z(0, 0)
-        quant_z(0, 1)
+        weigh(0, 0, 0, BANK)
+        quant_z(0)
+        quant_a(0, 0, 0)
+        all_bids(0, 1)
 
         for g in range(1, GROUPS):
+            turn_and_drain_x("s", g, 0, 2)
+            turn_and_drain_x("s", g, 2, 2)
+            if g == 1:
+                weigh(0, 1, 0, BANK)
+                quant_x(g, 0)
+                quant_x(g, 2)
+                all_costs(0, CE0)
+            else:
+                weigh(g - 1, 0, 0, BANK)
+                quant_c(g - 1)
+                quant_x(g, 0)
+                quant_x(g, 2)
+                quant_a(g - 1, 0, 0)
+                all_bids(g - 1, 1)
             for pair in range(2):
                 turn_and_drain_z("s", g, pair)
-            weigh(g - 1, 0, 0, HALF)
-            weigh(g - 1, 0, HALF, HALF)
-            quant_z(g, 0)
-            quant_z(g, 1)
-            quant_a(g - 1, 0, 0)
-            quant_a(g - 1, 0, HALF)
-            for t in range(PACK):
-                bids(g - 1, 1, t)
-            for t in range(PACK):
-                turn_and_drain_x("s", g, t)
-            weigh(g - 1, 1, 0, HALF)
-            quant_x(g, 0)
-            quant_x(g, 1)
+            if g > 1:
+                weigh(g - 1, 1, 0, HALF)
+            quant_z(g)
             if g == 1:
-                for cc in range(C_TILES):
-                    drain_costs("s", 0, cc, costs(0, cc))
-            weigh(g - 1, 1, HALF, HALF)
-            for cc in range(C_TILES):
-                if cc == 1:
-                    quant_x(g, 2)
-                    quant_x(g, 3)
-                drain_costs("v" if cc % 2 else "s", g, cc, costs(g, cc))
-            quant_a(g - 1, 1, 0)
-            quant_a(g - 1, 1, HALF)
-            if g == 1:
+                quant_a(0, 1, 0)
                 quant_c(0)
-            quant_c(g)
-            for t in range(PACK):
-                bids(g, 0, t)
+            else:
+                weigh(g - 1, 1, HALF, HALF)
+                quant_a(g - 1, 1, 0)
+                quant_a(g - 1, 1, HALF)
+            all_bids(g, 0)
+            all_costs(g, CE[g])
 
         weigh(last, 0, 0, HALF)
-        weigh(last, 0, HALF, HALF)
+        quant_c(last)
         quant_a(last, 0, 0)
-        quant_a(last, 0, HALF)
-        for t in range(PACK):
-            bids(last, 1, t)
-        banks = [new_bank(), new_bank()]
-        for j in range(2):
-            for g in range(last):
+        weigh(last, 0, HALF, HALF)
+        all_bids(last, 1)
+        banks = {}
+
+        def spend(j, groups):
+            if j not in banks:
+                banks[j] = new_bank()
+            for g in groups:
                 spend_pass(banks[j], j, g)
-        for j in range(HALVES * A_TILES):
-            if j < A_TILES:
-                weigh(last, 1, j * P, P)
-            if 0 < j <= A_TILES:
-                quant_a(last, 1, (j - 1) * P)
-            bank = banks[j] if j < 2 else new_bank()
-            for g in range(last if j < 2 else 0, GROUPS):
-                spend_pass(bank, j, g)
-            finish(bank, j)
+
+        spend(0, range(last))
+        spend(1, range(last))
+        spend(0, [last])
+        spend(1, [last])
+        quant_a(last, 0, HALF)
+        finish(banks[0], 0)
+        weigh(last, 1, 0, HALF)
+        spend(2, range(GROUPS))
+        finish(banks[1], 1)
+        quant_a(last, 1, 0)
+        spend(3, range(GROUPS))
+        weigh(last, 1, HALF, HALF)
+        finish(banks[2], 2)
+        quant_a(last, 1, HALF)
+        finish(banks[3], 3)
+        for j in range(A_TILES, HALVES * A_TILES - 1):
+            spend(j, range(GROUPS))
+            finish(banks[j], j)
+        j = HALVES * A_TILES - 1
+        for c0 in range(0, C, C // 2):
+            bank = new_bank()
+            for g in range(GROUPS):
+                spend_pass(bank, j, g, c0, C // 2)
+            finish(bank, j, c0, C // 2)

from contextlib import ExitStack

import concourse.mybir as mybir
from concourse.masks import make_identity

I, A, K, F, C = 2048, 1024, 1024, 512, 512
FLOPS = 2 * I * K * A + 2 * I * F * C + 2 * I * A * C

F32 = mybir.dt.float32
BF16 = mybir.dt.bfloat16
U32 = mybir.dt.uint32
I32 = mybir.dt.int32
U8 = mybir.dt.uint8
FP8X4 = mybir.dt.float8_e4m3fn_x4
FP4X4 = mybir.dt.float4_e2m1fn_x4
EXP = mybir.ActivationFunctionType.Exp
MULT = mybir.AluOpType.mult
SUB = mybir.AluOpType.subtract

P = 128
PACK = 4
PASS = P * PACK
BANK = 512
GROUPS = I // PASS
K_PASSES = K // PASS
HALVES = A // BANK
A_TILES = BANK // P
C_TILES = C // P
RUN = 4
CE0 = "svsv"
CE = ["", "svsv", "svsv", "svss"]


def tile_ad_allocation_dual_s11_kernel(tc, x, w_words, w_scales, discount, z, v, budget, out):
    nc = tc.nc
    with ExitStack() as ctx:
        keep = ctx.enter_context(tc.tile_pool(name="keep", bufs=1))
        stage = ctx.enter_context(tc.tile_pool(name="stage", bufs=4))
        psum = ctx.enter_context(tc.psum_pool(name="psum", bufs=8))
        ctx.enter_context(tc.manual_schedule())

        def kept(name, shape, dtype):
            return keep.tile(shape, dtype, name=name, align_bytes=64)

        def staged(name, shape, dtype, bufs):
            return stage.tile(shape, dtype, name=name, bufs=bufs, align_bytes=64)

        def new_bank():
            return psum.tile([P, BANK], F32, name="bank")

        def quantize(name, grouped, bufs=1):
            width = grouped.shape[1] // PACK
            codes = staged(name + "_codes", [P, width], U32, bufs)
            scales = staged(name + "_scales", [P, width], U8, bufs)
            nc.vector.quantize_mx(out=codes[:].bitcast(FP8X4), scales=scales[:], in_=grouped)
            return codes, scales

        ident = kept("ident", [P, P], F32)
        make_identity(nc, ident[:])
        w_plane = kept("w_plane", [P, K_PASSES * A], U8)
        nc.vector.memset(w_plane[:].bitcast(I32), 0)

        x_raw, z_raw, d_raw, w_raw, b_raw = {}, {}, {}, {}, {}
        x_rows = x.rearrange("(g m t) k -> g m t k", m=P, t=PACK)
        z_rows = z.rearrange("(g m t) f -> g m t f", m=P, t=PACK)
        d_rows = discount.rearrange("(g m t) a -> g m t a", m=P, t=PACK)

        def load_x(g, t0, n):
            raw = kept("x_raw%d_%d" % (g, t0), [P, n, K], BF16)
            nc.sync.dma_start(out=raw[:], in_=x_rows[g, :, t0:t0 + n, :])
            for t in range(n):
                x_raw[g, t0 + t] = raw[:, t, :]

        def load_z(g):
            z_raw[g] = kept("z_raw%d" % g, [P, PACK, F], BF16)
            nc.sync.dma_start(out=z_raw[g][:], in_=z_rows[g])

        def load_d(g, h):
            d_raw[g, h] = kept("d_raw%d_%d" % (g, h), [P, PACK, BANK], BF16)
            nc.sync.dma_start(out=d_raw[g, h][:], in_=d_rows[g, :, :, h * BANK:(h + 1) * BANK])

        def load_w(h):
            w_raw[h] = kept("w_raw%d" % h, [P, K_PASSES, 2 * BANK], U8)
            src = w_words.rearrange("g p n -> p g n")[:, :, 2 * h * BANK:2 * (h + 1) * BANK]
            nc.sync.dma_start(out=w_raw[h][:].bitcast(I32), in_=src.bitcast(I32))

        def load_w_scales():
            src = w_scales.rearrange("g (q r) n -> r q g n", r=PACK)
            for r in range(PACK):
                dst = w_plane[r:P:32, :].rearrange("q (g n) -> q g n", g=K_PASSES)
                nc.sync.dma_start(out=dst.bitcast(I32), in_=src[r].bitcast(I32))

        def load_budget(h):
            b_raw[h] = kept("b_raw%d" % h, [P, A_TILES, C], BF16)
            src = budget[h * BANK:(h + 1) * BANK, :].rearrange("(j m) c -> m j c", m=P)
            nc.sync.dma_start(out=b_raw[h][:], in_=src)

        load_x(0, 0, 1)
        load_x(0, 1, 1)
        load_x(0, 2, 1)
        load_x(0, 3, 1)
        load_w(0)
        load_w_scales()
        v_raw = kept("v_raw", [P, PACK, C], BF16)
        nc.sync.dma_start(out=v_raw[:], in_=v.rearrange("(p j) c -> p j c", j=PACK))
        load_z(0)
        load_d(0, 0)
        load_w(1)
        for g in range(1, GROUPS):
            load_x(g, 0, 2)
            load_x(g, 2, 2)
            load_d(g - 1, 1)
            load_z(g)
            load_d(g, 0)
        load_d(GROUPS - 1, 1)
        load_budget(0)
        load_budget(1)

        xq, zq, cq, aq = {}, {}, {}, {}
        x_grp, z_grp, c_grp, e_val, a_grp = {}, {}, {}, {}, {}

        def copy_on(engine, out_ap, in_ap):
            if engine == "s":
                nc.scalar.copy(out=out_ap, in_=in_ap)
            else:
                nc.vector.tensor_copy(out=out_ap, in_=in_ap)

        def turn_x(g, t):
            bank = new_bank()
            words = x_raw[g, t].bitcast(F32)
            for kp in range(K_PASSES):
                for u in range(2):
                    n = 2 * kp + u
                    nc.tensor.transpose(bank[:, n * P:(n + 1) * P], words[:, 256 * kp + u:256 * (kp + 1):2], ident[:])
            return bank

        def turn_z(g, pair):
            bank = new_bank()
            words = z_raw[g][:].rearrange("p t f -> p (t f)").bitcast(F32)
            for tt in range(2):
                t = 2 * pair + tt
                for u in range(2):
                    n = 2 * tt + u
                    nc.tensor.transpose(bank[:, n * P:(n + 1) * P], words[:, 256 * t + u:256 * (t + 1):2], ident[:])
            return bank

        def drain_words(engine, bank, grouped):
            copy_on(engine, grouped.bitcast(F32).rearrange("p (n m u) -> p n m u", n=2, u=2),
                    bank[:].rearrange("p (n u m) -> p n m u", n=2, u=2))

        def quant_x(g, t0):
            codes, scales = quantize("xq%d_%d" % (g, t0), x_grp[g, t0][:])
            width = K_PASSES * P
            for c0 in range(0, codes.shape[1], width):
                xq[g, t0 + c0 // width] = (codes[:, c0:c0 + width], scales[:, c0:c0 + width])

        def quant_z(g):
            zq[g] = quantize("zq", z_grp[g][:], 2)

        def bids(g, h, t):
            bank = new_bank()
            codes, scales = xq[g, t]
            for kp in range(K_PASSES):
                cols = slice(kp * P, (kp + 1) * P)
                nc.tensor.matmul_mx(
                    out=bank[:], lhsT=codes[:, cols].bitcast(FP8X4), lhsT_scale=scales[:, cols],
                    rhs=w_raw[h][:, kp, :].bitcast(FP4X4),
                    rhs_scale=w_plane[:, kp * A + h * BANK:kp * A + (h + 1) * BANK],
                    start=(kp == 0), stop=(kp == K_PASSES - 1))
            if t == 0:
                e_val[g, h] = staged("e_val", [P, PACK, BANK], F32, 3)
            nc.scalar.activation(out=e_val[g, h][:, t, :], in_=bank[:], func=EXP)

        def weigh(g, h, a0, n):
            grouped = staged("a_grp", [P, n * PACK], BF16, 3)
            a_grp[g, h, a0] = grouped
            nc.vector.tensor_tensor(
                out=grouped[:].rearrange("p (c i t) -> p c t i", i=RUN, t=PACK),
                in0=e_val[g, h][:, :, a0:a0 + n].rearrange("p t (c i) -> p c t i", i=RUN),
                in1=d_raw[g, h][:, :, a0:a0 + n].rearrange("p t (c i) -> p c t i", i=RUN),
                op=MULT)

        def quant_a(g, h, a0):
            codes, scales = quantize("aq%d_%d_%d" % (g, h, a0), a_grp[g, h, a0][:])
            for m0 in range(0, codes.shape[1], P):
                aq[g, (h * BANK + a0 + m0) // P] = (codes[:, m0:m0 + P], scales[:, m0:m0 + P])

        def costs(g, cc):
            bank = new_bank()
            v_codes, v_scales = vq
            cols = slice(cc * P, (cc + 1) * P)
            for t in range(PACK):
                codes, scales = zq[g]
                rows = slice(t * P, (t + 1) * P)
                nc.tensor.matmul_mx(
                    out=bank[:, t * P:(t + 1) * P], lhsT=codes[:, rows].bitcast(FP8X4), lhsT_scale=scales[:, rows],
                    rhs=v_codes[:, cols].bitcast(FP8X4), rhs_scale=v_scales[:, cols], start=True, stop=True)
            return bank

        def drain_costs(engine, g, cc, bank):
            if cc == 0:
                c_grp[g] = staged("c_grp", [P, C * PACK], BF16, 2)
            copy_on(engine, c_grp[g][:, cc * BANK:(cc + 1) * BANK].rearrange("p (n t) -> p n t", t=PACK),
                    bank[:].rearrange("p (t n) -> p n t", t=PACK))

        def quant_c(g):
            cq[g] = quantize("cq%d" % g, c_grp[g][:])

        def spend_pass(bank, j, g, c0=0, n=C):
            a_codes, a_scales = aq[g, j]
            c_codes, c_scales = cq[g]
            nc.tensor.matmul_mx(
                out=bank[:, 0:n], lhsT=a_codes.bitcast(FP8X4), lhsT_scale=a_scales,
                rhs=c_codes[:, c0:c0 + n].bitcast(FP8X4), rhs_scale=c_scales[:, c0:c0 + n],
                start=(g == 0), stop=(g == GROUPS - 1))

        def finish(bank, j, c0=0, n=C):
            res = staged("res", [P, n], F32, 8)
            nc.vector.tensor_tensor(out=res[:], in0=bank[:, 0:n], in1=b_raw[j // A_TILES][:, j % A_TILES, c0:c0 + n], op=SUB)
            nc.sync.dma_start(out=out[j * P:(j + 1) * P, c0:c0 + n], in_=res[:])

        HALF = BANK // 2
        last = GROUPS - 1

        def turn_and_drain_x(engine, g, t0, n):
            x_grp[g, t0] = staged("grp", [P, n * K], BF16, 4)
            for t in range(n):
                drain_words(engine, turn_x(g, t0 + t), x_grp[g, t0][:, t * K:(t + 1) * K])

        def turn_and_drain_z(engine, g, pair):
            if pair == 0:
                z_grp[g] = staged("grp", [P, 4 * BANK], BF16, 4)
            drain_words(engine, turn_z(g, pair), z_grp[g][:, pair * 2 * BANK:(pair + 1) * 2 * BANK])

        def all_bids(g, h):
            for t in range(PACK):
                bids(g, h, t)

        def all_costs(g, engines):
            for cc in range(C_TILES):
                drain_costs(engines[cc], g, cc, costs(g, cc))

        for t in range(PACK):
            turn_and_drain_x("v", 0, t, 1)
            if t % 2:
                quant_x(0, t - 1)
                quant_x(0, t)
        all_bids(0, 0)
        v_grp = staged("grp", [P, C * PACK], BF16, 4)
        nc.vector.tensor_copy(
            out=v_grp[:].rearrange("p (c i t) -> p c t i", i=RUN, t=PACK),
            in_=v_raw[:].rearrange("p t (c i) -> p c t i", i=RUN))
        turn_and_drain_z("s", 0, 0)
        turn_and_drain_z("s", 0, 1)
        vq = quantize("vq", v_grp[:])
        weigh(0, 0, 0, BANK)
        quant_z(0)
        quant_a(0, 0, 0)
        all_bids(0, 1)

        for g in range(1, GROUPS):
            turn_and_drain_x("s", g, 0, 2)
            turn_and_drain_x("s", g, 2, 2)
            if g == 1:
                weigh(0, 1, 0, BANK)
                quant_x(g, 0)
                quant_x(g, 2)
                all_costs(0, CE0)
            else:
                weigh(g - 1, 0, 0, BANK)
                quant_c(g - 1)
                quant_x(g, 0)
                quant_x(g, 2)
                quant_a(g - 1, 0, 0)
                all_bids(g - 1, 1)
            for pair in range(2):
                turn_and_drain_z("s", g, pair)
            if g > 1:
                weigh(g - 1, 1, 0, HALF)
            quant_z(g)
            if g == 1:
                quant_a(0, 1, 0)
                quant_c(0)
            else:
                weigh(g - 1, 1, HALF, HALF)
                quant_a(g - 1, 1, 0)
                quant_a(g - 1, 1, HALF)
            all_bids(g, 0)
            all_costs(g, CE[g])

        weigh(last, 0, 0, HALF)
        quant_c(last)
        quant_a(last, 0, 0)
        weigh(last, 0, HALF, HALF)
        all_bids(last, 1)
        banks = {}

        def spend(j, groups):
            if j not in banks:
                banks[j] = new_bank()
            for g in groups:
                spend_pass(banks[j], j, g)

        spend(0, range(last))
        spend(1, range(last))
        spend(0, [last])
        spend(1, [last])
        quant_a(last, 0, HALF)
        finish(banks[0], 0)
        weigh(last, 1, 0, HALF)
        spend(2, range(GROUPS))
        finish(banks[1], 1)
        quant_a(last, 1, 0)
        spend(3, range(GROUPS))
        weigh(last, 1, HALF, HALF)
        finish(banks[2], 2)
        quant_a(last, 1, HALF)
        finish(banks[3], 3)
        for j in range(A_TILES, HALVES * A_TILES - 1):
            spend(j, range(GROUPS))
            finish(banks[j], j)
        j = HALVES * A_TILES - 1
        for c0 in range(0, C, C // 2):
            bank = new_bank()
            for g in range(GROUPS):
                spend_pass(bank, j, g, c0, C // 2)
            finish(bank, j, c0, C // 2)
